import numpy as np
import ml_dtypes


def mxq(x, axis, fmt="e4m3"):
    dtype, down = {"e4m3": (ml_dtypes.float8_e4m3fn, 7), "e5m2": (ml_dtypes.float8_e5m2, 14)}[fmt]
    v = np.moveaxis(np.asarray(x, np.float32).astype(ml_dtypes.bfloat16).astype(np.float64), axis, -1)
    blocks = v.reshape(v.shape[:-1] + (-1, 32))
    amax = np.abs(blocks).max(-1, keepdims=True)
    byte = np.maximum(np.where(amax > 0, np.frexp(amax)[1] - 1 + 127, 0) - down, 1)
    scale = np.exp2(byte - 127.0)
    codes = (blocks / scale).astype(np.float32).astype(dtype).astype(np.float64)
    return np.moveaxis((codes * scale).reshape(v.shape), -1, axis)


WIDE = False


def mx_kscale(k):
    if not WIDE:
        return np.ones(k)
    levels = np.array([30, -30])
    if k % 512:
        return np.exp2(np.random.permutation(np.resize(levels, k // 32))).repeat(32)
    a = np.empty((k // 512, 16))
    for p in range(k // 512):
        a[p, :8] = np.random.permutation(np.resize(levels, 8))
        for g in range(8):
            far = levels[np.abs(levels - a[p, g]) >= 10]
            a[p, g + 8] = far[np.random.randint(len(far))]
    return np.exp2(a.ravel()).repeat(32)


BF16 = ml_dtypes.bfloat16


def bf(x):
    return np.asarray(x, np.float32).astype(BF16)


def f64(x):
    return np.asarray(x).astype(np.float64)


E2M1 = np.array([0.0, 0.5, 1.0, 1.5, 2.0, 3.0, 4.0, 6.0, -0.0, -0.5, -1.0, -1.5, -2.0, -3.0, -4.0, -6.0])


def pack_weight(w, fmt):
    k, n = w.shape
    w = f64(bf(w)).reshape(k // 32, 32, n)
    amax = np.abs(w).max(1)
    if fmt == "e4m3":
        byte = np.frexp(amax)[1] - 1 + 127 - 7
    else:
        mant, ex = np.frexp(amax / 6.0)
        byte = np.where(mant > 0.5, ex, ex - 1) + 127
    byte = np.clip(np.where(amax > 0, byte, 1), 1, 254)
    scaled = (w * np.exp2(127.0 - byte)[:, None, :]).reshape(k, n).astype(np.float32)
    by_word = np.ascontiguousarray(scaled.reshape(k // 512, 128, 4, n).transpose(0, 1, 3, 2))
    if fmt == "e4m3":
        words = by_word.astype(ml_dtypes.float8_e4m3fn).view(np.uint8)
    else:
        c = by_word.astype(ml_dtypes.float4_e2m1fn).view(np.uint8) & 0xF
        words = c[..., 0::2] | (c[..., 1::2] << 4)
    return np.ascontiguousarray(words), np.ascontiguousarray(byte.astype(np.uint8).reshape(k // 512, 16, n))


def unpack_weight(words, scales, fmt):
    g, p, n, _ = words.shape
    if fmt == "e4m3":
        vals = np.ascontiguousarray(words).view(ml_dtypes.float8_e4m3fn).astype(np.float64)
    else:
        nib = np.empty((g, p, n, 4), np.uint8)
        nib[..., 0::2] = words & 0xF
        nib[..., 1::2] = words >> 4
        vals = E2M1[nib]
    vals = vals * np.repeat(np.exp2(scales.astype(np.float64) - 127.0), 8, axis=1)[..., None]
    return vals.transpose(0, 1, 3, 2).reshape(g * 512, n)
def pack4(w):
    words, scales = pack_weight(w, "e2m1")
    return words.reshape(words.shape[0], 128, -1), scales


def unpack4(words, scales):
    return unpack_weight(words.reshape(words.shape[0], 128, -1, 2), scales, "e2m1")


K, M, G, R = 1024, 1024, 2048, 512


def setup_inputs():
    s, t = mx_kscale(K), mx_kscale(G)
    d = np.random.standard_normal((K, G)) * 0.8 / np.sqrt(K) / s[:, None]
    d_words, d_scales = pack4(d)
    return {"ranges": bf(np.random.standard_normal((K, M)) * s[:, None]),
            "d_words": d_words,
            "d_scales": d_scales,
            "prior": bf(np.exp(0.3 * np.random.standard_normal(G)) * t),
            "fuse": bf(np.random.standard_normal((R, G)) / np.sqrt(G) / t),
            "zone_bias": bf(0.3 * np.random.standard_normal(R))}


def reference(ranges, d_words, d_scales, prior, fuse, zone_bias):
    d = unpack4(d_words, d_scales)
    r = mxq(f64(ranges), 0, "e4m3")
    loglik = d.T @ r
    post = np.exp(loglik) * f64(prior)[:, None]
    f = mxq(f64(fuse), 1, "e4m3")
    zones = f @ mxq(post, 0, "e5m2")
    return zones + f64(zone_bias)[:, None]

@@ -1,0 +1,308 @@
+from contextlib import ExitStack
+
+import concourse.mybir as mybir
+from concourse.masks import make_identity
+
+K, M, G, R = 1024, 1024, 2048, 512
+FLOPS = 2 * K * G * M + 2 * G * R * M
+
+F32 = mybir.dt.float32
+BF16 = mybir.dt.bfloat16
+I32 = mybir.dt.int32
+U32 = mybir.dt.uint32
+U8 = mybir.dt.uint8
+E4M3 = mybir.dt.float8_e4m3fn_x4
+E5M2 = mybir.dt.float8_e5m2_x4
+E2M1 = mybir.dt.float4_e2m1fn_x4
+ACT = mybir.ActivationFunctionType
+ALU = mybir.AluOpType
+
+P = 128
+PACK = 4
+N = 512
+K_PASSES = K // 512
+CELL_PASSES = G // 512
+HALVES = M // N
+ZONE_TILES = R // P
+LN_LOW = 2.0 ** -62
+LN_HIGH = 2.0 ** 64
+
+
+def tile_multistatic_grid_fusion_s9_kernel(tc, ranges, d_words, d_scales, prior, fuse, zone_bias, out):
+    nc = tc.nc
+    with ExitStack() as ctx:
+        keep = ctx.enter_context(tc.tile_pool(name="keep", bufs=1))
+        turn = ctx.enter_context(tc.tile_pool(name="turn", bufs=1))
+        psum = ctx.enter_context(tc.psum_pool(name="psum", bufs=1))
+        ctx.enter_context(tc.manual_schedule())
+
+        d_words32 = d_words.bitcast(I32)
+        d_scales32 = d_scales.bitcast(I32)
+        out_z = out.rearrange("(p c) m -> p c m", c=ZONE_TILES)
+        fuse_z = fuse.rearrange("(p c) k -> p c k", c=ZONE_TILES)
+
+        prior_rows = keep.tile([P, 512], BF16, name="prior_rows")
+        ident_bf = keep.tile([P, P], BF16, name="ident_bf")
+        ident_f32 = keep.tile([P, P], F32, name="ident_f32")
+        warm = keep.tile([P, 1], F32, name="warm")
+        warm_out = keep.tile([P, 1], F32, name="warm_out")
+        prior_parts = keep.tile([P, 3, 16], F32, name="prior_parts")
+        ln_parts = keep.tile([P, 3, 16], F32, name="ln_parts")
+        ln_prior = keep.tile([P, 16], F32, name="ln_prior")
+        bias = keep.tile([P, ZONE_TILES], BF16, name="bias")
+        sraw_first = keep.tile([P, K_PASSES, 128], I32, name="sraw_first")
+        sraw_rest = keep.tile([P, K_PASSES, 384], I32, name="sraw_rest")
+        s_first = keep.tile([P, K_PASSES * 512], U8, name="s_first", align_bytes=64)
+        s_rest = keep.tile([P, K_PASSES * 1536], U8, name="s_rest", align_bytes=64)
+
+        d_raw, d_sorted, r_raw, r_codes, r_scales = {}, {}, {}, {}, {}
+        f_raw, f_words, f_grouped, f_codes, f_scales = {}, {}, {}, {}, {}
+        grouped, post, p_codes, p_scales, banks, f_banks = {}, {}, {}, {}, {}, {}
+
+        def load_scales(queue, raw, w0, w1):
+            for q in range(4):
+                queue.dma_start(out=raw[32 * q : 32 * q + 4, :, :],
+                                in_=d_scales32[:, 4 * q : 4 * q + 4, w0:w1].rearrange("g r w -> r g w"))
+
+        def load_d(c):
+            d_raw[c] = keep.tile([P, K_PASSES, 256], I32, name="d_raw%d" % c)
+            nc.sync.dma_start(out=d_raw[c][:], in_=d_words32[:, :, 256 * c : 256 * (c + 1)].rearrange("g p w -> p g w"))
+
+        def load_ranges(g, h):
+            r_raw[g, h] = keep.tile([P, PACK, N], BF16, name="r_raw%d%d" % (g, h))
+            nc.sync.dma_start(out=r_raw[g, h][:],
+                              in_=ranges[512 * g : 512 * (g + 1), N * h : N * (h + 1)].rearrange("(p j) m -> p j m", j=PACK))
+
+        def load_fuse(z):
+            f_raw[z] = keep.tile([P, G], BF16, name="f_raw%d" % z)
+            nc.sync.dma_start(out=f_raw[z][:], in_=fuse_z[:, z, :])
+
+        def sort_d(c):
+            d_sorted[c] = keep.tile([P, K_PASSES * 1024], U8, name="d_sorted%d" % c, align_bytes=64)
+            nc.vector.tensor_copy(
+                out=d_sorted[c][:].bitcast(I32).rearrange("p (g t q w) -> p g t q w", g=K_PASSES, t=PACK, q=16),
+                in_=d_raw[c][:].rearrange("p g (q t w) -> p g t q w", q=16, t=PACK))
+
+        def sort_scales(raw, dst):
+            nc.vector.tensor_copy(
+                out=dst[:].bitcast(I32).rearrange("p (a t q w) -> p a t q w", t=PACK, q=16, w=2),
+                in_=raw[:].rearrange("p g (c q t w) -> p (g c) t q w", q=16, t=PACK, w=2))
+
+        def d_operand(c, g, t):
+            codes = d_sorted[c][:, 1024 * g + 256 * t : 1024 * g + 256 * (t + 1)].bitcast(E2M1)
+            if c == 0:
+                lo = 512 * g + 128 * t
+                return codes, s_first[:, lo : lo + 128]
+            lo = 1536 * g + 512 * (c - 1) + 128 * t
+            return codes, s_rest[:, lo : lo + 128]
+
+        def new_grouped(key):
+            grouped[key] = turn.tile([P, N, PACK], BF16, name="grouped", tag="grouped", bufs=4, align_bytes=64)
+
+        def interleave(engine, key, src, c0, c1):
+            dst = grouped[key][:, c0:c1, :].rearrange("p (c i) t -> p c t i", i=4)
+            rows = src[:, :, c0:c1].rearrange("p t (c i) -> p c t i", i=4)
+            if engine == "scalar":
+                nc.scalar.copy(out=dst, in_=rows)
+            else:
+                nc.vector.tensor_copy(out=dst, in_=rows)
+
+        def quantize(key, codes, scales, fmt):
+            codes[key] = keep.tile([P, N], U32, name="codes_%s%d" % key, align_bytes=64)
+            scales[key] = keep.tile([P, N], U8, name="scales_%s%d" % key, align_bytes=64)
+            nc.vector.quantize_mx(out=codes[key][:].bitcast(fmt), scales=scales[key][:],
+                                  in_=grouped[key][:].rearrange("p n t -> p (n t)"))
+
+        def group_ranges(g, h):
+            new_grouped(("r", 2 * h + g))
+            interleave("vector", ("r", 2 * h + g), r_raw[g, h], 0, N)
+
+        def quantize_ranges(g, h):
+            quantize(("r", 2 * h + g), r_codes, r_scales, E4M3)
+
+        def group_post(u):
+            new_grouped(("p", u))
+            interleave("vector", ("p", u), post[u], 0, N)
+
+        def quantize_post(u):
+            quantize(("p", u), p_codes, p_scales, E5M2)
+
+        def pair_fuse(z):
+            f_words[z] = turn.tile([P, G], BF16, name="f_words", tag="f_words", bufs=2)
+            nc.vector.tensor_copy(out=f_words[z][:].rearrange("p (u b r e) -> p u b r e", u=2, r=8, e=2),
+                                  in_=f_raw[z][:].rearrange("p (b u e r) -> p u b r e", u=2, e=2, r=8))
+
+        def transpose_fuse(z):
+            words = f_words[z][:].bitcast(F32)
+            for half in range(2):
+                tag = "b%d" % ((2 * z + half + 1) % 4)
+                bank = psum.tile([P, 2, 2, P], F32, name=tag, tag=tag)
+                f_banks[z, half] = bank
+                for j in range(2):
+                    for u in range(2):
+                        lo = 512 * u + P * (2 * half + j)
+                        nc.tensor.transpose(bank[:, j, u, :], words[:, lo : lo + P], ident_f32[:])
+
+        def copy_fuse(z):
+            f_grouped[z] = keep.tile([P, G], BF16, name="f_grouped%d" % z, align_bytes=64)
+            words = f_grouped[z][:].bitcast(F32).rearrange("p (c n u) -> p c n u", c=CELL_PASSES, u=2)
+            for half in range(2):
+                nc.scalar.copy(out=words[:, 2 * half : 2 * half + 2, :, :],
+                               in_=f_banks[z, half][:].rearrange("p c u n -> p c n u"))
+
+        def quantize_fuse(z):
+            f_codes[z] = keep.tile([P, 512], U32, name="f_codes%d" % z, align_bytes=64)
+            f_scales[z] = keep.tile([P, 512], U8, name="f_scales%d" % z, align_bytes=64)
+            nc.vector.quantize_mx(out=f_codes[z][:].bitcast(E4M3), scales=f_scales[z][:], in_=f_grouped[z][:])
+
+        def loglik_pass(u, t, g):
+            h, c = divmod(u, CELL_PASSES)
+            if g == 0:
+                banks[u, t] = psum.tile([P, N], F32, name="a%d" % t, tag="a%d" % t)
+            codes, scales = d_operand(c, g, t)
+            key = ("r", 2 * h + g)
+            nc.tensor.matmul_mx(out=banks[u, t][:], lhsT=codes, lhsT_scale=scales,
+                                rhs=r_codes[key][:].bitcast(E4M3), rhs_scale=r_scales[key][:],
+                                start=(g == 0), stop=(g == K_PASSES - 1))
+
+        def posterior(u, t):
+            c = u % CELL_PASSES
+            if t == 0:
+                post[u] = keep.tile([P, PACK, N], BF16, name="post%d" % u)
+            col = PACK * c + t
+            nc.scalar.activation(out=post[u][:, t, :], in_=banks[u, t][:], func=ACT.Exp,
+                                 bias=ln_prior[:, col : col + 1], scale=1.0)
+
+        def unit(u):
+            for t in range(PACK):
+                for g in range(K_PASSES):
+                    loglik_pass(u, t, g)
+                posterior(u, t)
+
+        def zones_pass(h, z, c):
+            if c == 0:
+                tag = ("b%d" if h == 0 else "a%d") % z
+                banks["o", h, z] = psum.tile([P, N], F32, name=tag, tag=tag)
+            key = ("p", CELL_PASSES * h + c)
+            nc.tensor.matmul_mx(out=banks["o", h, z][:],
+                                lhsT=f_codes[z][:, P * c : P * (c + 1)].bitcast(E4M3),
+                                lhsT_scale=f_scales[z][:, P * c : P * (c + 1)],
+                                rhs=p_codes[key][:].bitcast(E5M2), rhs_scale=p_scales[key][:],
+                                start=(c == 0), stop=(c == CELL_PASSES - 1))
+
+        def finish(engine, h, z):
+            result = keep.tile([P, N], F32, name="result%d%d" % (h, z))
+            if engine == "scalar":
+                nc.scalar.activation(out=result[:], in_=banks["o", h, z][:], func=ACT.Identity,
+                                     bias=bias[:, z : z + 1], scale=1.0)
+            else:
+                nc.vector.tensor_scalar(out=result[:], in0=banks["o", h, z][:], scalar1=bias[:, z : z + 1],
+                                        scalar2=None, op0=ALU.add)
+            nc.sync.dma_start(out=out_z[:, z, N * h : N * (h + 1)], in_=result[:])
+
+        nc.gpsimd.memset(prior_rows[:].bitcast(I32), 0)
+        nc.vector.memset(sraw_first[:], 0)
+        nc.vector.memset(warm[:], 1.0)
+        nc.vector.memset(sraw_rest[:], 0)
+        make_identity(nc, ident_bf[:])
+        make_identity(nc, ident_f32[:])
+
+        load_d(0)
+        load_ranges(0, 0)
+        load_ranges(1, 0)
+        nc.scalar.dma_start(out=prior_rows[0:PACK, :].rearrange("t (b r) -> t b r", r=8),
+                            in_=prior.rearrange("(b t r) -> t b r", t=PACK, r=8))
+        load_scales(nc.scalar, sraw_first, 0, 128)
+        nc.scalar.activation(out=warm_out[:], in_=warm[:], func=ACT.Ln)
+        load_d(1)
+        load_scales(nc.sync, sraw_rest, 128, 512)
+        load_fuse(0)
+        load_d(2)
+        load_d(3)
+        load_ranges(0, 1)
+        load_fuse(1)
+        load_ranges(1, 1)
+        load_fuse(2)
+        load_fuse(3)
+        nc.sync.dma_start(out=bias[:], in_=zone_bias.rearrange("(p c) -> p c", c=ZONE_TILES))
+
+        sort_d(0)
+        sort_scales(sraw_first, s_first)
+        new_grouped(("r", 0))
+        interleave("scalar", ("r", 0), r_raw[0, 0], 0, 160)
+        interleave("vector", ("r", 0), r_raw[0, 0], 160, N)
+
+        prior_bank = psum.tile([P, CELL_PASSES, P], BF16, name="b0", tag="b0")
+        for c in range(CELL_PASSES):
+            nc.tensor.transpose(prior_bank[:, c, :], prior_rows[:, P * c : P * (c + 1)], ident_bf[:])
+        cells = prior_bank[:, :, 0:PACK]
+        parts = prior_parts[:].rearrange("p a (c t) -> p a c t", t=PACK)
+        nc.vector.tensor_scalar(out=parts[:, 0, :, :], in0=cells, scalar1=LN_LOW, scalar2=LN_HIGH, op0=ALU.max, op1=ALU.min)
+        nc.vector.tensor_scalar(out=parts[:, 1, :, :], in0=cells, scalar1=LN_LOW, scalar2=1.0 / LN_LOW, op0=ALU.min, op1=ALU.mult)
+        nc.vector.tensor_scalar(out=parts[:, 2, :, :], in0=cells, scalar1=LN_HIGH, scalar2=1.0 / LN_HIGH, op0=ALU.max, op1=ALU.mult)
+        nc.scalar.activation(out=ln_parts[:], in_=prior_parts[:], func=ACT.Ln)
+        nc.scalar.activation(out=warm_out[:], in_=warm[:], func=ACT.Exp)
+
+        quantize_ranges(0, 0)
+        group_ranges(1, 0)
+        nc.vector.tensor_reduce(out=ln_prior[:], in_=ln_parts[:].rearrange("p a n -> p n a"), axis=mybir.AxisListType.X, op=ALU.add)
+        quantize_ranges(1, 0)
+        for g in range(K_PASSES):
+            for t in range(PACK):
+                loglik_pass(0, t, g)
+        for t in range(PACK):
+            posterior(0, t)
+
+        sort_d(1)
+        sort_scales(sraw_rest, s_rest)
+        unit(1)
+        pair_fuse(0)
+        sort_d(2)
+        sort_d(3)
+        transpose_fuse(0)
+        copy_fuse(0)
+        unit(2)
+        group_ranges(0, 1)
+        pair_fuse(1)
+        quantize_ranges(0, 1)
+        transpose_fuse(1)
+        copy_fuse(1)
+        unit(3)
+        group_ranges(1, 1)
+        quantize_fuse(0)
+        quantize_ranges(1, 1)
+        unit(4)
+        group_post(0)
+        pair_fuse(2)
+        quantize_post(0)
+        transpose_fuse(2)
+        copy_fuse(2)
+        unit(5)
+        group_post(1)
+        quantize_fuse(1)
+        quantize_post(1)
+        pair_fuse(3)
+        transpose_fuse(3)
+        copy_fuse(3)
+        unit(6)
+        unit(7)
+        group_post(2)
+        quantize_fuse(2)
+        quantize_post(2)
+        group_post(3)
+        quantize_fuse(3)
+        group_post(4)
+        quantize_post(3)
+        for z in range(ZONE_TILES):
+            for c in range(CELL_PASSES):
+                zones_pass(0, z, c)
+            finish("scalar", 0, z)
+        for c in range(CELL_PASSES):
+            u = CELL_PASSES + c
+            if c + 1 < CELL_PASSES:
+                group_post(u + 1)
+            quantize_post(u)
+            for z in range(ZONE_TILES):
+                zones_pass(1, z, c)
+        for z in range(ZONE_TILES):
+            finish("vector" if z % 2 == 0 else "scalar", 1, z)

@@ -59,6 +59,13 @@ def tile_multistatic_grid_fusion_s9_kernel(tc, ranges, d_words, d_scales, prior,
         f_raw, f_words, f_grouped, f_codes, f_scales = {}, {}, {}, {}, {}
         grouped, post, p_codes, p_scales, banks, f_banks = {}, {}, {}, {}, {}, {}
 
+        bank_count = []
+
+        def next_bank(shape, dtype):
+            tag = "bank%d" % (len(bank_count) % 8)
+            bank_count.append(tag)
+            return psum.tile(shape, dtype, name=tag, tag=tag)
+
         def load_scales(queue, raw, w0, w1):
             for q in range(4):
                 queue.dma_start(out=raw[32 * q : 32 * q + 4, :, :],
@@ -128,15 +135,14 @@ def tile_multistatic_grid_fusion_s9_kernel(tc, ranges, d_words, d_scales, prior,
             quantize(("p", u), p_codes, p_scales, E5M2)
 
         def pair_fuse(z):
-            f_words[z] = turn.tile([P, G], BF16, name="f_words", tag="f_words", bufs=2)
+            f_words[z] = turn.tile([P, G], BF16, name="f_words", tag="f_words", bufs=3)
             nc.vector.tensor_copy(out=f_words[z][:].rearrange("p (u b r e) -> p u b r e", u=2, r=8, e=2),
                                   in_=f_raw[z][:].rearrange("p (b u e r) -> p u b r e", u=2, e=2, r=8))
 
         def transpose_fuse(z):
             words = f_words[z][:].bitcast(F32)
             for half in range(2):
-                tag = "b%d" % ((2 * z + half + 1) % 4)
-                bank = psum.tile([P, 2, 2, P], F32, name=tag, tag=tag)
+                bank = next_bank([P, 2, 2, P], F32)
                 f_banks[z, half] = bank
                 for j in range(2):
                     for u in range(2):
@@ -158,7 +164,7 @@ def tile_multistatic_grid_fusion_s9_kernel(tc, ranges, d_words, d_scales, prior,
         def loglik_pass(u, t, g):
             h, c = divmod(u, CELL_PASSES)
             if g == 0:
-                banks[u, t] = psum.tile([P, N], F32, name="a%d" % t, tag="a%d" % t)
+                banks[u, t] = next_bank([P, N], F32)
             codes, scales = d_operand(c, g, t)
             key = ("r", 2 * h + g)
             nc.tensor.matmul_mx(out=banks[u, t][:], lhsT=codes, lhsT_scale=scales,
@@ -181,8 +187,7 @@ def tile_multistatic_grid_fusion_s9_kernel(tc, ranges, d_words, d_scales, prior,
 
         def zones_pass(h, z, c):
             if c == 0:
-                tag = ("b%d" if h == 0 else "a%d") % z
-                banks["o", h, z] = psum.tile([P, N], F32, name=tag, tag=tag)
+                banks["o", h, z] = next_bank([P, N], F32)
             key = ("p", CELL_PASSES * h + c)
             nc.tensor.matmul_mx(out=banks["o", h, z][:],
                                 lhsT=f_codes[z][:, P * c : P * (c + 1)].bitcast(E4M3),
@@ -200,41 +205,43 @@ def tile_multistatic_grid_fusion_s9_kernel(tc, ranges, d_words, d_scales, prior,
                                         scalar2=None, op0=ALU.add)
             nc.sync.dma_start(out=out_z[:, z, N * h : N * (h + 1)], in_=result[:])
 
-        nc.gpsimd.memset(prior_rows[:].bitcast(I32), 0)
+        nc.vector.memset(prior_rows[:].bitcast(I32), 0)
         nc.vector.memset(sraw_first[:], 0)
         nc.vector.memset(warm[:], 1.0)
         nc.vector.memset(sraw_rest[:], 0)
         make_identity(nc, ident_bf[:])
-        make_identity(nc, ident_f32[:])
-
-        load_d(0)
-        load_ranges(0, 0)
-        load_ranges(1, 0)
-        nc.scalar.dma_start(out=prior_rows[0:PACK, :].rearrange("t (b r) -> t b r", r=8),
-                            in_=prior.rearrange("(b t r) -> t b r", t=PACK, r=8))
-        load_scales(nc.scalar, sraw_first, 0, 128)
         nc.scalar.activation(out=warm_out[:], in_=warm[:], func=ACT.Ln)
+        nc.scalar.copy(out=ident_f32[:], in_=ident_bf[:])
+
+        load_ranges(0, 0)
+        load_d(0)
+        nc.sync.dma_start(out=prior_rows[0:PACK, :].rearrange("t (b r) -> t b r", r=8),
+                          in_=prior.rearrange("(b t r) -> t b r", t=PACK, r=8))
+        load_scales(nc.sync, sraw_first, 0, 128)
+        load_ranges(1, 0)
         load_d(1)
         load_scales(nc.sync, sraw_rest, 128, 512)
         load_fuse(0)
         load_d(2)
+        load_fuse(1)
         load_d(3)
         load_ranges(0, 1)
-        load_fuse(1)
-        load_ranges(1, 1)
         load_fuse(2)
+        load_ranges(1, 1)
         load_fuse(3)
         nc.sync.dma_start(out=bias[:], in_=zone_bias.rearrange("(p c) -> p c", c=ZONE_TILES))
 
-        sort_d(0)
-        sort_scales(sraw_first, s_first)
+        prior_bank = next_bank([P, CELL_PASSES, P], BF16)
+        for c in range(CELL_PASSES):
+            nc.tensor.transpose(prior_bank[:, c, :], prior_rows[:, P * c : P * (c + 1)], ident_bf[:])
+
         new_grouped(("r", 0))
         interleave("scalar", ("r", 0), r_raw[0, 0], 0, 160)
         interleave("vector", ("r", 0), r_raw[0, 0], 160, N)
+        sort_d(0)
+        sort_scales(sraw_first, s_first)
+        quantize_ranges(0, 0)
 
-        prior_bank = psum.tile([P, CELL_PASSES, P], BF16, name="b0", tag="b0")
-        for c in range(CELL_PASSES):
-            nc.tensor.transpose(prior_bank[:, c, :], prior_rows[:, P * c : P * (c + 1)], ident_bf[:])
         cells = prior_bank[:, :, 0:PACK]
         parts = prior_parts[:].rearrange("p a (c t) -> p a c t", t=PACK)
         nc.vector.tensor_scalar(out=parts[:, 0, :, :], in0=cells, scalar1=LN_LOW, scalar2=LN_HIGH, op0=ALU.max, op1=ALU.min)
@@ -243,7 +250,6 @@ def tile_multistatic_grid_fusion_s9_kernel(tc, ranges, d_words, d_scales, prior,
         nc.scalar.activation(out=ln_parts[:], in_=prior_parts[:], func=ACT.Ln)
         nc.scalar.activation(out=warm_out[:], in_=warm[:], func=ACT.Exp)
 
-        quantize_ranges(0, 0)
         group_ranges(1, 0)
         nc.vector.tensor_reduce(out=ln_prior[:], in_=ln_parts[:].rearrange("p a n -> p n a"), axis=mybir.AxisListType.X, op=ALU.add)
         quantize_ranges(1, 0)
@@ -258,51 +264,52 @@ def tile_multistatic_grid_fusion_s9_kernel(tc, ranges, d_words, d_scales, prior,
         unit(1)
         pair_fuse(0)
         sort_d(2)
-        sort_d(3)
         transpose_fuse(0)
         copy_fuse(0)
         unit(2)
-        group_ranges(0, 1)
         pair_fuse(1)
-        quantize_ranges(0, 1)
+        sort_d(3)
         transpose_fuse(1)
         copy_fuse(1)
         unit(3)
-        group_ranges(1, 1)
-        quantize_fuse(0)
-        quantize_ranges(1, 1)
-        unit(4)
-        group_post(0)
+        group_ranges(0, 1)
         pair_fuse(2)
-        quantize_post(0)
+        quantize_ranges(0, 1)
         transpose_fuse(2)
         copy_fuse(2)
-        unit(5)
-        group_post(1)
-        quantize_fuse(1)
-        quantize_post(1)
+        group_ranges(1, 1)
         pair_fuse(3)
+        quantize_ranges(1, 1)
+        unit(4)
         transpose_fuse(3)
         copy_fuse(3)
+        unit(5)
         unit(6)
         unit(7)
-        group_post(2)
-        quantize_fuse(2)
-        quantize_post(2)
-        group_post(3)
-        quantize_fuse(3)
+        for u in range(CELL_PASSES):
+            group_post(u)
+            quantize_fuse(u)
+            quantize_post(u)
         group_post(4)
-        quantize_post(3)
+        group_post(5)
+        quantize_post(4)
+        group_post(6)
+        quantize_post(5)
         for z in range(ZONE_TILES):
             for c in range(CELL_PASSES):
                 zones_pass(0, z, c)
+        finish("scalar", 0, 0)
+        new_grouped(("p", 7))
+        interleave("scalar", ("p", 7), post[7], 0, 256)
+        interleave("vector", ("p", 7), post[7], 256, N)
+        for z in range(1, ZONE_TILES):
             finish("scalar", 0, z)
-        for c in range(CELL_PASSES):
-            u = CELL_PASSES + c
-            if c + 1 < CELL_PASSES:
-                group_post(u + 1)
-            quantize_post(u)
+        quantize_post(6)
+        quantize_post(7)
+        for c in range(2):
             for z in range(ZONE_TILES):
                 zones_pass(1, z, c)
         for z in range(ZONE_TILES):
+            for c in range(2, CELL_PASSES):
+                zones_pass(1, z, c)
             finish("vector" if z % 2 == 0 else "scalar", 1, z)

@@ -41,6 +41,7 @@ def tile_multistatic_grid_fusion_s9_kernel(tc, ranges, d_words, d_scales, prior,
         out_z = out.rearrange("(p c) m -> p c m", c=ZONE_TILES)
         fuse_z = fuse.rearrange("(p c) k -> p c k", c=ZONE_TILES)
 
+        prior_raw = keep.tile([CELL_PASSES, 512], BF16, name="prior_raw")
         prior_rows = keep.tile([P, 512], BF16, name="prior_rows")
         ident_bf = keep.tile([P, P], BF16, name="ident_bf")
         ident_f32 = keep.tile([P, P], F32, name="ident_f32")
@@ -66,9 +67,9 @@ def tile_multistatic_grid_fusion_s9_kernel(tc, ranges, d_words, d_scales, prior,
             bank_count.append(tag)
             return psum.tile(shape, dtype, name=tag, tag=tag)
 
-        def load_scales(queue, raw, w0, w1):
+        def load_scales(queues, raw, w0, w1):
             for q in range(4):
-                queue.dma_start(out=raw[32 * q : 32 * q + 4, :, :],
+                queues[q].dma_start(out=raw[32 * q : 32 * q + 4, :, :],
                                 in_=d_scales32[:, 4 * q : 4 * q + 4, w0:w1].rearrange("g r w -> r g w"))
 
         def load_d(c):
@@ -90,10 +91,10 @@ def tile_multistatic_grid_fusion_s9_kernel(tc, ranges, d_words, d_scales, prior,
                 out=d_sorted[c][:].bitcast(I32).rearrange("p (g t q w) -> p g t q w", g=K_PASSES, t=PACK, q=16),
                 in_=d_raw[c][:].rearrange("p g (q t w) -> p g t q w", q=16, t=PACK))
 
-        def sort_scales(raw, dst):
+        def sort_scales(raw, dst, rows):
             nc.vector.tensor_copy(
-                out=dst[:].bitcast(I32).rearrange("p (a t q w) -> p a t q w", t=PACK, q=16, w=2),
-                in_=raw[:].rearrange("p g (c q t w) -> p (g c) t q w", q=16, t=PACK, w=2))
+                out=dst[rows, :].bitcast(I32).rearrange("p (a t q w) -> p a t q w", t=PACK, q=16, w=2),
+                in_=raw[rows, :, :].rearrange("p g (c q t w) -> p (g c) t q w", q=16, t=PACK, w=2))
 
         def d_operand(c, g, t):
             codes = d_sorted[c][:, 1024 * g + 256 * t : 1024 * g + 256 * (t + 1)].bitcast(E2M1)
@@ -135,7 +136,7 @@ def tile_multistatic_grid_fusion_s9_kernel(tc, ranges, d_words, d_scales, prior,
             quantize(("p", u), p_codes, p_scales, E5M2)
 
         def pair_fuse(z):
-            f_words[z] = turn.tile([P, G], BF16, name="f_words", tag="f_words", bufs=3)
+            f_words[z] = turn.tile([P, G], BF16, name="f_words", tag="f_words", bufs=2)
             nc.vector.tensor_copy(out=f_words[z][:].rearrange("p (u b r e) -> p u b r e", u=2, r=8, e=2),
                                   in_=f_raw[z][:].rearrange("p (b u e r) -> p u b r e", u=2, e=2, r=8))
 
@@ -175,7 +176,7 @@ def tile_multistatic_grid_fusion_s9_kernel(tc, ranges, d_words, d_scales, prior,
             c = u % CELL_PASSES
             if t == 0:
                 post[u] = keep.tile([P, PACK, N], BF16, name="post%d" % u)
-            col = PACK * c + t
+            col = CELL_PASSES * t + c
             nc.scalar.activation(out=post[u][:, t, :], in_=banks[u, t][:], func=ACT.Exp,
                                  bias=ln_prior[:, col : col + 1], scale=1.0)
 
@@ -195,55 +196,59 @@ def tile_multistatic_grid_fusion_s9_kernel(tc, ranges, d_words, d_scales, prior,
                                 rhs=p_codes[key][:].bitcast(E5M2), rhs_scale=p_scales[key][:],
                                 start=(c == 0), stop=(c == CELL_PASSES - 1))
 
-        def finish(engine, h, z):
-            result = keep.tile([P, N], F32, name="result%d%d" % (h, z))
-            if engine == "scalar":
-                nc.scalar.activation(out=result[:], in_=banks["o", h, z][:], func=ACT.Identity,
-                                     bias=bias[:, z : z + 1], scale=1.0)
-            else:
-                nc.vector.tensor_scalar(out=result[:], in0=banks["o", h, z][:], scalar1=bias[:, z : z + 1],
-                                        scalar2=None, op0=ALU.add)
-            nc.sync.dma_start(out=out_z[:, z, N * h : N * (h + 1)], in_=result[:])
+        def finish(engine, h, z, pieces=1):
+            width = N // pieces
+            for lo in range(0, N, width):
+                result = keep.tile([P, width], F32, name="result%d%d_%d" % (h, z, lo))
+                sums = banks["o", h, z][:, lo : lo + width]
+                if engine == "scalar":
+                    nc.scalar.activation(out=result[:], in_=sums, func=ACT.Identity, bias=bias[:, z : z + 1], scale=1.0)
+                else:
+                    nc.vector.tensor_scalar(out=result[:], in0=sums, scalar1=bias[:, z : z + 1], scalar2=None, op0=ALU.add)
+                nc.sync.dma_start(out=out_z[:, z, N * h + lo : N * h + lo + width], in_=result[:])
+
+        nc.scalar.dma_start(out=prior_raw[:], in_=prior.rearrange("(c n) -> c n", c=CELL_PASSES))
+        load_scales([nc.sync, nc.scalar, nc.sync, nc.scalar], sraw_first, 0, 128)
+        load_ranges(0, 0)
+        load_d(0)
+        load_ranges(1, 0)
 
         nc.vector.memset(prior_rows[:].bitcast(I32), 0)
-        nc.vector.memset(sraw_first[:], 0)
         nc.vector.memset(warm[:], 1.0)
+        nc.vector.memset(s_first[:].bitcast(I32), 0)
         nc.vector.memset(sraw_rest[:], 0)
         make_identity(nc, ident_bf[:])
         nc.scalar.activation(out=warm_out[:], in_=warm[:], func=ACT.Ln)
         nc.scalar.copy(out=ident_f32[:], in_=ident_bf[:])
 
-        load_ranges(0, 0)
-        load_d(0)
-        nc.sync.dma_start(out=prior_rows[0:PACK, :].rearrange("t (b r) -> t b r", r=8),
-                          in_=prior.rearrange("(b t r) -> t b r", t=PACK, r=8))
-        load_scales(nc.sync, sraw_first, 0, 128)
-        load_ranges(1, 0)
         load_d(1)
-        load_scales(nc.sync, sraw_rest, 128, 512)
+        load_scales([nc.sync] * 4, sraw_rest, 128, 512)
         load_fuse(0)
         load_d(2)
         load_fuse(1)
         load_d(3)
         load_ranges(0, 1)
-        load_fuse(2)
         load_ranges(1, 1)
+        load_fuse(2)
         load_fuse(3)
         nc.sync.dma_start(out=bias[:], in_=zone_bias.rearrange("(p c) -> p c", c=ZONE_TILES))
 
-        prior_bank = next_bank([P, CELL_PASSES, P], BF16)
-        for c in range(CELL_PASSES):
-            nc.tensor.transpose(prior_bank[:, c, :], prior_rows[:, P * c : P * (c + 1)], ident_bf[:])
+        nc.vector.tensor_copy(out=prior_rows[0:CELL_PASSES, :].rearrange("c (t q r) -> c t q r", t=PACK, r=8),
+                              in_=prior_raw[:].rearrange("c (q t r) -> c t q r", t=PACK, r=8))
+        for q in range(4):
+            sort_scales(sraw_first, s_first, slice(32 * q, 32 * q + 4))
+        prior_bank = next_bank([P, PACK, P], BF16)
+        for t in range(PACK):
+            nc.tensor.transpose(prior_bank[:, t, :], prior_rows[:, P * t : P * (t + 1)], ident_bf[:])
 
         new_grouped(("r", 0))
         interleave("scalar", ("r", 0), r_raw[0, 0], 0, 160)
         interleave("vector", ("r", 0), r_raw[0, 0], 160, N)
         sort_d(0)
-        sort_scales(sraw_first, s_first)
         quantize_ranges(0, 0)
 
-        cells = prior_bank[:, :, 0:PACK]
-        parts = prior_parts[:].rearrange("p a (c t) -> p a c t", t=PACK)
+        cells = prior_bank[:, :, 0:CELL_PASSES]
+        parts = prior_parts[:].rearrange("p a (t c) -> p a t c", t=PACK)
         nc.vector.tensor_scalar(out=parts[:, 0, :, :], in0=cells, scalar1=LN_LOW, scalar2=LN_HIGH, op0=ALU.max, op1=ALU.min)
         nc.vector.tensor_scalar(out=parts[:, 1, :, :], in0=cells, scalar1=LN_LOW, scalar2=1.0 / LN_LOW, op0=ALU.min, op1=ALU.mult)
         nc.vector.tensor_scalar(out=parts[:, 2, :, :], in0=cells, scalar1=LN_HIGH, scalar2=1.0 / LN_HIGH, op0=ALU.max, op1=ALU.mult)
@@ -260,28 +265,28 @@ def tile_multistatic_grid_fusion_s9_kernel(tc, ranges, d_words, d_scales, prior,
             posterior(0, t)
 
         sort_d(1)
-        sort_scales(sraw_rest, s_rest)
+        sort_scales(sraw_rest, s_rest, slice(0, P))
         unit(1)
         pair_fuse(0)
         sort_d(2)
-        transpose_fuse(0)
-        copy_fuse(0)
         unit(2)
         pair_fuse(1)
         sort_d(3)
+        transpose_fuse(0)
         transpose_fuse(1)
+        copy_fuse(0)
         copy_fuse(1)
         unit(3)
         group_ranges(0, 1)
-        pair_fuse(2)
-        quantize_ranges(0, 1)
-        transpose_fuse(2)
-        copy_fuse(2)
         group_ranges(1, 1)
-        pair_fuse(3)
+        quantize_ranges(0, 1)
+        pair_fuse(2)
         quantize_ranges(1, 1)
+        pair_fuse(3)
         unit(4)
+        transpose_fuse(2)
         transpose_fuse(3)
+        copy_fuse(2)
         copy_fuse(3)
         unit(5)
         unit(6)
@@ -300,8 +305,8 @@ def tile_multistatic_grid_fusion_s9_kernel(tc, ranges, d_words, d_scales, prior,
                 zones_pass(0, z, c)
         finish("scalar", 0, 0)
         new_grouped(("p", 7))
-        interleave("scalar", ("p", 7), post[7], 0, 256)
-        interleave("vector", ("p", 7), post[7], 256, N)
+        interleave("scalar", ("p", 7), post[7], 0, 128)
+        interleave("vector", ("p", 7), post[7], 128, N)
         for z in range(1, ZONE_TILES):
             finish("scalar", 0, z)
         quantize_post(6)
@@ -312,4 +317,4 @@ def tile_multistatic_grid_fusion_s9_kernel(tc, ranges, d_words, d_scales, prior,
         for z in range(ZONE_TILES):
             for c in range(2, CELL_PASSES):
                 zones_pass(1, z, c)
-            finish("vector" if z % 2 == 0 else "scalar", 1, z)
+            finish("vector" if z % 2 == 0 else "scalar", 1, z, 2 if z == ZONE_TILES - 1 else 1)

@@ -20,6 +20,7 @@ ALU = mybir.AluOpType
 P = 128
 PACK = 4
 N = 512
+PIECE = 256
 K_PASSES = K // 512
 CELL_PASSES = G // 512
 HALVES = M // N
@@ -45,8 +46,6 @@ def tile_multistatic_grid_fusion_s9_kernel(tc, ranges, d_words, d_scales, prior,
         prior_rows = keep.tile([P, 512], BF16, name="prior_rows")
         ident_bf = keep.tile([P, P], BF16, name="ident_bf")
         ident_f32 = keep.tile([P, P], F32, name="ident_f32")
-        warm = keep.tile([P, 1], F32, name="warm")
-        warm_out = keep.tile([P, 1], F32, name="warm_out")
         prior_parts = keep.tile([P, 3, 16], F32, name="prior_parts")
         ln_parts = keep.tile([P, 3, 16], F32, name="ln_parts")
         ln_prior = keep.tile([P, 16], F32, name="ln_prior")
@@ -67,10 +66,9 @@ def tile_multistatic_grid_fusion_s9_kernel(tc, ranges, d_words, d_scales, prior,
             bank_count.append(tag)
             return psum.tile(shape, dtype, name=tag, tag=tag)
 
-        def load_scales(queues, raw, w0, w1):
-            for q in range(4):
-                queues[q].dma_start(out=raw[32 * q : 32 * q + 4, :, :],
-                                in_=d_scales32[:, 4 * q : 4 * q + 4, w0:w1].rearrange("g r w -> r g w"))
+        def load_scales(raw, w0, w1):
+            for r in range(4):
+                nc.sync.dma_start(out=raw[r:P:32, :, :], in_=d_scales32[:, r:16:4, w0:w1].rearrange("g q w -> q g w"))
 
         def load_d(c):
             d_raw[c] = keep.tile([P, K_PASSES, 256], I32, name="d_raw%d" % c)
@@ -80,6 +78,26 @@ def tile_multistatic_grid_fusion_s9_kernel(tc, ranges, d_words, d_scales, prior,
             r_raw[g, h] = keep.tile([P, PACK, N], BF16, name="r_raw%d%d" % (g, h))
             nc.sync.dma_start(out=r_raw[g, h][:],
                               in_=ranges[512 * g : 512 * (g + 1), N * h : N * (h + 1)].rearrange("(p j) m -> p j m", j=PACK))
+
+        def load_piece(g, a):
+            r_raw["a", g, a] = keep.tile([P, PACK, PIECE], BF16, name="r_piece%d%d" % (g, a))
+            nc.sync.dma_start(out=r_raw["a", g, a][:],
+                              in_=ranges[512 * g : 512 * (g + 1), PIECE * a : PIECE * (a + 1)].rearrange("(p j) m -> p j m", j=PACK))
+
+        def group_piece(g, a, scalar_columns):
+            grouped["a", g, a] = keep.tile([P, PIECE, PACK], BF16, name="grouped_piece%d%d" % (g, a), align_bytes=64)
+            if scalar_columns:
+                interleave("scalar", ("a", g, a), r_raw["a", g, a], 0, scalar_columns)
+            interleave("vector", ("a", g, a), r_raw["a", g, a], scalar_columns, PIECE)
+
+        def quantize_piece(g, a):
+            key = ("r", g)
+            if a == 0:
+                r_codes[key] = keep.tile([P, N], U32, name="codes_r%d" % g, align_bytes=64)
+                r_scales[key] = keep.tile([P, N], U8, name="scales_r%d" % g, align_bytes=64)
+            cols = slice(PIECE * a, PIECE * (a + 1))
+            nc.vector.quantize_mx(out=r_codes[key][:, cols].bitcast(E4M3), scales=r_scales[key][:, cols],
+                                  in_=grouped["a", g, a][:].rearrange("p n t -> p (n t)"))
 
         def load_fuse(z):
             f_raw[z] = keep.tile([P, G], BF16, name="f_raw%d" % z)
@@ -91,10 +109,10 @@ def tile_multistatic_grid_fusion_s9_kernel(tc, ranges, d_words, d_scales, prior,
                 out=d_sorted[c][:].bitcast(I32).rearrange("p (g t q w) -> p g t q w", g=K_PASSES, t=PACK, q=16),
                 in_=d_raw[c][:].rearrange("p g (q t w) -> p g t q w", q=16, t=PACK))
 
-        def sort_scales(raw, dst, rows):
+        def sort_scales(raw, dst):
             nc.vector.tensor_copy(
-                out=dst[rows, :].bitcast(I32).rearrange("p (a t q w) -> p a t q w", t=PACK, q=16, w=2),
-                in_=raw[rows, :, :].rearrange("p g (c q t w) -> p (g c) t q w", q=16, t=PACK, w=2))
+                out=dst[:].bitcast(I32).rearrange("p (a t q w) -> p a t q w", t=PACK, q=16, w=2),
+                in_=raw[:].rearrange("p g (c q t w) -> p (g c) t q w", q=16, t=PACK, w=2))
 
         def d_operand(c, g, t):
             codes = d_sorted[c][:, 1024 * g + 256 * t : 1024 * g + 256 * (t + 1)].bitcast(E2M1)
@@ -207,22 +225,19 @@ def tile_multistatic_grid_fusion_s9_kernel(tc, ranges, d_words, d_scales, prior,
                     nc.vector.tensor_scalar(out=result[:], in0=sums, scalar1=bias[:, z : z + 1], scalar2=None, op0=ALU.add)
                 nc.sync.dma_start(out=out_z[:, z, N * h + lo : N * h + lo + width], in_=result[:])
 
-        nc.scalar.dma_start(out=prior_raw[:], in_=prior.rearrange("(c n) -> c n", c=CELL_PASSES))
-        load_scales([nc.sync, nc.scalar, nc.sync, nc.scalar], sraw_first, 0, 128)
-        load_ranges(0, 0)
-        load_d(0)
-        load_ranges(1, 0)
-
+        nc.vector.memset(sraw_first[:], 0)
         nc.vector.memset(prior_rows[:].bitcast(I32), 0)
-        nc.vector.memset(warm[:], 1.0)
-        nc.vector.memset(s_first[:].bitcast(I32), 0)
         nc.vector.memset(sraw_rest[:], 0)
         make_identity(nc, ident_bf[:])
-        nc.scalar.activation(out=warm_out[:], in_=warm[:], func=ACT.Ln)
-        nc.scalar.copy(out=ident_f32[:], in_=ident_bf[:])
 
+        nc.sync.dma_start(out=prior_raw[:], in_=prior.rearrange("(c n) -> c n", c=CELL_PASSES))
+        load_piece(0, 0)
+        load_piece(0, 1)
+        load_d(0)
+        load_scales(sraw_first, 0, 128)
+        load_ranges(1, 0)
         load_d(1)
-        load_scales([nc.sync] * 4, sraw_rest, 128, 512)
+        load_scales(sraw_rest, 128, 512)
         load_fuse(0)
         load_d(2)
         load_fuse(1)
@@ -235,26 +250,24 @@ def tile_multistatic_grid_fusion_s9_kernel(tc, ranges, d_words, d_scales, prior,
 
         nc.vector.tensor_copy(out=prior_rows[0:CELL_PASSES, :].rearrange("c (t q r) -> c t q r", t=PACK, r=8),
                               in_=prior_raw[:].rearrange("c (q t r) -> c t q r", t=PACK, r=8))
-        for q in range(4):
-            sort_scales(sraw_first, s_first, slice(32 * q, 32 * q + 4))
         prior_bank = next_bank([P, PACK, P], BF16)
         for t in range(PACK):
             nc.tensor.transpose(prior_bank[:, t, :], prior_rows[:, P * t : P * (t + 1)], ident_bf[:])
 
-        new_grouped(("r", 0))
-        interleave("scalar", ("r", 0), r_raw[0, 0], 0, 160)
-        interleave("vector", ("r", 0), r_raw[0, 0], 160, N)
+        group_piece(0, 0, 0)
+        group_piece(0, 1, 96)
+        quantize_piece(0, 0)
         sort_d(0)
-        quantize_ranges(0, 0)
-
+        quantize_piece(0, 1)
+        sort_scales(sraw_first, s_first)
         cells = prior_bank[:, :, 0:CELL_PASSES]
         parts = prior_parts[:].rearrange("p a (t c) -> p a t c", t=PACK)
         nc.vector.tensor_scalar(out=parts[:, 0, :, :], in0=cells, scalar1=LN_LOW, scalar2=LN_HIGH, op0=ALU.max, op1=ALU.min)
         nc.vector.tensor_scalar(out=parts[:, 1, :, :], in0=cells, scalar1=LN_LOW, scalar2=1.0 / LN_LOW, op0=ALU.min, op1=ALU.mult)
         nc.vector.tensor_scalar(out=parts[:, 2, :, :], in0=cells, scalar1=LN_HIGH, scalar2=1.0 / LN_HIGH, op0=ALU.max, op1=ALU.mult)
         nc.scalar.activation(out=ln_parts[:], in_=prior_parts[:], func=ACT.Ln)
-        nc.scalar.activation(out=warm_out[:], in_=warm[:], func=ACT.Exp)
 
+        nc.scalar.copy(out=ident_f32[:], in_=ident_bf[:])
         group_ranges(1, 0)
         nc.vector.tensor_reduce(out=ln_prior[:], in_=ln_parts[:].rearrange("p a n -> p n a"), axis=mybir.AxisListType.X, op=ALU.add)
         quantize_ranges(1, 0)
@@ -265,7 +278,7 @@ def tile_multistatic_grid_fusion_s9_kernel(tc, ranges, d_words, d_scales, prior,
             posterior(0, t)
 
         sort_d(1)
-        sort_scales(sraw_rest, s_rest, slice(0, P))
+        sort_scales(sraw_rest, s_rest)
         unit(1)
         pair_fuse(0)
         sort_d(2)

from contextlib import ExitStack

import concourse.mybir as mybir
from concourse.masks import make_identity

K, M, G, R = 1024, 1024, 2048, 512
FLOPS = 2 * K * G * M + 2 * G * R * M

F32 = mybir.dt.float32
BF16 = mybir.dt.bfloat16
I32 = mybir.dt.int32
U32 = mybir.dt.uint32
U8 = mybir.dt.uint8
E4M3 = mybir.dt.float8_e4m3fn_x4
E5M2 = mybir.dt.float8_e5m2_x4
E2M1 = mybir.dt.float4_e2m1fn_x4
ACT = mybir.ActivationFunctionType
ALU = mybir.AluOpType

P = 128
PACK = 4
N = 512
PIECE = 256
K_PASSES = K // 512
CELL_PASSES = G // 512
HALVES = M // N
ZONE_TILES = R // P
LN_LOW = 2.0 ** -62
LN_HIGH = 2.0 ** 64


def tile_multistatic_grid_fusion_s9_kernel(tc, ranges, d_words, d_scales, prior, fuse, zone_bias, out):
    nc = tc.nc
    with ExitStack() as ctx:
        keep = ctx.enter_context(tc.tile_pool(name="keep", bufs=1))
        turn = ctx.enter_context(tc.tile_pool(name="turn", bufs=1))
        psum = ctx.enter_context(tc.psum_pool(name="psum", bufs=1))
        ctx.enter_context(tc.manual_schedule())

        d_words32 = d_words.bitcast(I32)
        d_scales32 = d_scales.bitcast(I32)
        out_z = out.rearrange("(p c) m -> p c m", c=ZONE_TILES)
        fuse_z = fuse.rearrange("(p c) k -> p c k", c=ZONE_TILES)

        prior_raw = keep.tile([CELL_PASSES, 512], BF16, name="prior_raw")
        prior_rows = keep.tile([P, 512], BF16, name="prior_rows")
        ident_bf = keep.tile([P, P], BF16, name="ident_bf")
        ident_f32 = keep.tile([P, P], F32, name="ident_f32")
        prior_parts = keep.tile([P, 3, 16], F32, name="prior_parts")
        ln_parts = keep.tile([P, 3, 16], F32, name="ln_parts")
        ln_prior = keep.tile([P, 16], F32, name="ln_prior")
        bias = keep.tile([P, ZONE_TILES], BF16, name="bias")
        sraw_first = keep.tile([P, K_PASSES, 128], I32, name="sraw_first")
        sraw_rest = keep.tile([P, K_PASSES, 384], I32, name="sraw_rest")
        s_first = keep.tile([P, K_PASSES * 512], U8, name="s_first", align_bytes=64)
        s_rest = keep.tile([P, K_PASSES * 1536], U8, name="s_rest", align_bytes=64)

        d_raw, d_sorted, r_raw, r_codes, r_scales = {}, {}, {}, {}, {}
        f_raw, f_words, f_grouped, f_codes, f_scales = {}, {}, {}, {}, {}
        grouped, post, p_codes, p_scales, banks, f_banks = {}, {}, {}, {}, {}, {}

        bank_count = []

        def next_bank(shape, dtype):
            tag = "bank%d" % (len(bank_count) % 8)
            bank_count.append(tag)
            return psum.tile(shape, dtype, name=tag, tag=tag)

        def load_scales(raw, w0, w1):
            for r in range(4):
                nc.sync.dma_start(out=raw[r:P:32, :, :], in_=d_scales32[:, r:16:4, w0:w1].rearrange("g q w -> q g w"))

        def load_d(c):
            d_raw[c] = keep.tile([P, K_PASSES, 256], I32, name="d_raw%d" % c)
            nc.sync.dma_start(out=d_raw[c][:], in_=d_words32[:, :, 256 * c : 256 * (c + 1)].rearrange("g p w -> p g w"))

        def load_ranges(g, h):
            r_raw[g, h] = keep.tile([P, PACK, N], BF16, name="r_raw%d%d" % (g, h))
            nc.sync.dma_start(out=r_raw[g, h][:],
                              in_=ranges[512 * g : 512 * (g + 1), N * h : N * (h + 1)].rearrange("(p j) m -> p j m", j=PACK))

        def load_piece(g, a):
            r_raw["a", g, a] = keep.tile([P, PACK, PIECE], BF16, name="r_piece%d%d" % (g, a))
            nc.sync.dma_start(out=r_raw["a", g, a][:],
                              in_=ranges[512 * g : 512 * (g + 1), PIECE * a : PIECE * (a + 1)].rearrange("(p j) m -> p j m", j=PACK))

        def group_piece(g, a, scalar_columns):
            grouped["a", g, a] = keep.tile([P, PIECE, PACK], BF16, name="grouped_piece%d%d" % (g, a), align_bytes=64)
            if scalar_columns:
                interleave("scalar", ("a", g, a), r_raw["a", g, a], 0, scalar_columns)
            interleave("vector", ("a", g, a), r_raw["a", g, a], scalar_columns, PIECE)

        def quantize_piece(g, a):
            key = ("r", g)
            if a == 0:
                r_codes[key] = keep.tile([P, N], U32, name="codes_r%d" % g, align_bytes=64)
                r_scales[key] = keep.tile([P, N], U8, name="scales_r%d" % g, align_bytes=64)
            cols = slice(PIECE * a, PIECE * (a + 1))
            nc.vector.quantize_mx(out=r_codes[key][:, cols].bitcast(E4M3), scales=r_scales[key][:, cols],
                                  in_=grouped["a", g, a][:].rearrange("p n t -> p (n t)"))

        def load_fuse(z):
            f_raw[z] = keep.tile([P, G], BF16, name="f_raw%d" % z)
            nc.sync.dma_start(out=f_raw[z][:], in_=fuse_z[:, z, :])

        def sort_d(c):
            d_sorted[c] = keep.tile([P, K_PASSES * 1024], U8, name="d_sorted%d" % c, align_bytes=64)
            nc.vector.tensor_copy(
                out=d_sorted[c][:].bitcast(I32).rearrange("p (g t q w) -> p g t q w", g=K_PASSES, t=PACK, q=16),
                in_=d_raw[c][:].rearrange("p g (q t w) -> p g t q w", q=16, t=PACK))

        def sort_scales(raw, dst):
            nc.vector.tensor_copy(
                out=dst[:].bitcast(I32).rearrange("p (a t q w) -> p a t q w", t=PACK, q=16, w=2),
                in_=raw[:].rearrange("p g (c q t w) -> p (g c) t q w", q=16, t=PACK, w=2))

        def d_operand(c, g, t):
            codes = d_sorted[c][:, 1024 * g + 256 * t : 1024 * g + 256 * (t + 1)].bitcast(E2M1)
            if c == 0:
                lo = 512 * g + 128 * t
                return codes, s_first[:, lo : lo + 128]
            lo = 1536 * g + 512 * (c - 1) + 128 * t
            return codes, s_rest[:, lo : lo + 128]

        def new_grouped(key):
            grouped[key] = turn.tile([P, N, PACK], BF16, name="grouped", tag="grouped", bufs=4, align_bytes=64)

        def interleave(engine, key, src, c0, c1):
            dst = grouped[key][:, c0:c1, :].rearrange("p (c i) t -> p c t i", i=4)
            rows = src[:, :, c0:c1].rearrange("p t (c i) -> p c t i", i=4)
            if engine == "scalar":
                nc.scalar.copy(out=dst, in_=rows)
            else:
                nc.vector.tensor_copy(out=dst, in_=rows)

        def quantize(key, codes, scales, fmt):
            codes[key] = keep.tile([P, N], U32, name="codes_%s%d" % key, align_bytes=64)
            scales[key] = keep.tile([P, N], U8, name="scales_%s%d" % key, align_bytes=64)
            nc.vector.quantize_mx(out=codes[key][:].bitcast(fmt), scales=scales[key][:],
                                  in_=grouped[key][:].rearrange("p n t -> p (n t)"))

        def group_ranges(g, h):
            new_grouped(("r", 2 * h + g))
            interleave("vector", ("r", 2 * h + g), r_raw[g, h], 0, N)

        def quantize_ranges(g, h):
            quantize(("r", 2 * h + g), r_codes, r_scales, E4M3)

        def group_post(u):
            new_grouped(("p", u))
            interleave("vector", ("p", u), post[u], 0, N)

        def quantize_post(u):
            quantize(("p", u), p_codes, p_scales, E5M2)

        def pair_fuse(z):
            f_words[z] = turn.tile([P, G], BF16, name="f_words", tag="f_words", bufs=2)
            nc.vector.tensor_copy(out=f_words[z][:].rearrange("p (u b r e) -> p u b r e", u=2, r=8, e=2),
                                  in_=f_raw[z][:].rearrange("p (b u e r) -> p u b r e", u=2, e=2, r=8))

        def transpose_fuse(z):
            words = f_words[z][:].bitcast(F32)
            for half in range(2):
                bank = next_bank([P, 2, 2, P], F32)
                f_banks[z, half] = bank
                for j in range(2):
                    for u in range(2):
                        lo = 512 * u + P * (2 * half + j)
                        nc.tensor.transpose(bank[:, j, u, :], words[:, lo : lo + P], ident_f32[:])

        def copy_fuse(z):
            f_grouped[z] = keep.tile([P, G], BF16, name="f_grouped%d" % z, align_bytes=64)
            words = f_grouped[z][:].bitcast(F32).rearrange("p (c n u) -> p c n u", c=CELL_PASSES, u=2)
            for half in range(2):
                nc.scalar.copy(out=words[:, 2 * half : 2 * half + 2, :, :],
                               in_=f_banks[z, half][:].rearrange("p c u n -> p c n u"))

        def quantize_fuse(z):
            f_codes[z] = keep.tile([P, 512], U32, name="f_codes%d" % z, align_bytes=64)
            f_scales[z] = keep.tile([P, 512], U8, name="f_scales%d" % z, align_bytes=64)
            nc.vector.quantize_mx(out=f_codes[z][:].bitcast(E4M3), scales=f_scales[z][:], in_=f_grouped[z][:])

        def loglik_pass(u, t, g):
            h, c = divmod(u, CELL_PASSES)
            if g == 0:
                banks[u, t] = next_bank([P, N], F32)
            codes, scales = d_operand(c, g, t)
            key = ("r", 2 * h + g)
            nc.tensor.matmul_mx(out=banks[u, t][:], lhsT=codes, lhsT_scale=scales,
                                rhs=r_codes[key][:].bitcast(E4M3), rhs_scale=r_scales[key][:],
                                start=(g == 0), stop=(g == K_PASSES - 1))

        def posterior(u, t):
            c = u % CELL_PASSES
            if t == 0:
                post[u] = keep.tile([P, PACK, N], BF16, name="post%d" % u)
            col = CELL_PASSES * t + c
            nc.scalar.activation(out=post[u][:, t, :], in_=banks[u, t][:], func=ACT.Exp,
                                 bias=ln_prior[:, col : col + 1], scale=1.0)

        def unit(u):
            for t in range(PACK):
                for g in range(K_PASSES):
                    loglik_pass(u, t, g)
                posterior(u, t)

        def zones_pass(h, z, c):
            if c == 0:
                banks["o", h, z] = next_bank([P, N], F32)
            key = ("p", CELL_PASSES * h + c)
            nc.tensor.matmul_mx(out=banks["o", h, z][:],
                                lhsT=f_codes[z][:, P * c : P * (c + 1)].bitcast(E4M3),
                                lhsT_scale=f_scales[z][:, P * c : P * (c + 1)],
                                rhs=p_codes[key][:].bitcast(E5M2), rhs_scale=p_scales[key][:],
                                start=(c == 0), stop=(c == CELL_PASSES - 1))

        def finish(engine, h, z, pieces=1):
            width = N // pieces
            for lo in range(0, N, width):
                result = keep.tile([P, width], F32, name="result%d%d_%d" % (h, z, lo))
                sums = banks["o", h, z][:, lo : lo + width]
                if engine == "scalar":
                    nc.scalar.activation(out=result[:], in_=sums, func=ACT.Identity, bias=bias[:, z : z + 1], scale=1.0)
                else:
                    nc.vector.tensor_scalar(out=result[:], in0=sums, scalar1=bias[:, z : z + 1], scalar2=None, op0=ALU.add)
                nc.sync.dma_start(out=out_z[:, z, N * h + lo : N * h + lo + width], in_=result[:])

        nc.vector.memset(sraw_first[:], 0)
        nc.vector.memset(prior_rows[:].bitcast(I32), 0)
        nc.vector.memset(sraw_rest[:], 0)
        make_identity(nc, ident_bf[:])

        nc.sync.dma_start(out=prior_raw[:], in_=prior.rearrange("(c n) -> c n", c=CELL_PASSES))
        load_piece(0, 0)
        load_piece(0, 1)
        load_d(0)
        load_scales(sraw_first, 0, 128)
        load_ranges(1, 0)
        load_d(1)
        load_scales(sraw_rest, 128, 512)
        load_fuse(0)
        load_d(2)
        load_fuse(1)
        load_d(3)
        load_ranges(0, 1)
        load_ranges(1, 1)
        load_fuse(2)
        load_fuse(3)
        nc.sync.dma_start(out=bias[:], in_=zone_bias.rearrange("(p c) -> p c", c=ZONE_TILES))

        nc.vector.tensor_copy(out=prior_rows[0:CELL_PASSES, :].rearrange("c (t q r) -> c t q r", t=PACK, r=8),
                              in_=prior_raw[:].rearrange("c (q t r) -> c t q r", t=PACK, r=8))
        prior_bank = next_bank([P, PACK, P], BF16)
        for t in range(PACK):
            nc.tensor.transpose(prior_bank[:, t, :], prior_rows[:, P * t : P * (t + 1)], ident_bf[:])

        group_piece(0, 0, 0)
        group_piece(0, 1, 96)
        quantize_piece(0, 0)
        sort_d(0)
        quantize_piece(0, 1)
        sort_scales(sraw_first, s_first)
        cells = prior_bank[:, :, 0:CELL_PASSES]
        parts = prior_parts[:].rearrange("p a (t c) -> p a t c", t=PACK)
        nc.vector.tensor_scalar(out=parts[:, 0, :, :], in0=cells, scalar1=LN_LOW, scalar2=LN_HIGH, op0=ALU.max, op1=ALU.min)
        nc.vector.tensor_scalar(out=parts[:, 1, :, :], in0=cells, scalar1=LN_LOW, scalar2=1.0 / LN_LOW, op0=ALU.min, op1=ALU.mult)
        nc.vector.tensor_scalar(out=parts[:, 2, :, :], in0=cells, scalar1=LN_HIGH, scalar2=1.0 / LN_HIGH, op0=ALU.max, op1=ALU.mult)
        nc.scalar.activation(out=ln_parts[:], in_=prior_parts[:], func=ACT.Ln)

        nc.scalar.copy(out=ident_f32[:], in_=ident_bf[:])
        group_ranges(1, 0)
        nc.vector.tensor_reduce(out=ln_prior[:], in_=ln_parts[:].rearrange("p a n -> p n a"), axis=mybir.AxisListType.X, op=ALU.add)
        quantize_ranges(1, 0)
        for g in range(K_PASSES):
            for t in range(PACK):
                loglik_pass(0, t, g)
        for t in range(PACK):
            posterior(0, t)

        sort_d(1)
        sort_scales(sraw_rest, s_rest)
        unit(1)
        pair_fuse(0)
        sort_d(2)
        unit(2)
        pair_fuse(1)
        sort_d(3)
        transpose_fuse(0)
        transpose_fuse(1)
        copy_fuse(0)
        copy_fuse(1)
        unit(3)
        group_ranges(0, 1)
        group_ranges(1, 1)
        quantize_ranges(0, 1)
        pair_fuse(2)
        quantize_ranges(1, 1)
        pair_fuse(3)
        unit(4)
        transpose_fuse(2)
        transpose_fuse(3)
        copy_fuse(2)
        copy_fuse(3)
        unit(5)
        unit(6)
        unit(7)
        for u in range(CELL_PASSES):
            group_post(u)
            quantize_fuse(u)
            quantize_post(u)
        group_post(4)
        group_post(5)
        quantize_post(4)
        group_post(6)
        quantize_post(5)
        for z in range(ZONE_TILES):
            for c in range(CELL_PASSES):
                zones_pass(0, z, c)
        finish("scalar", 0, 0)
        new_grouped(("p", 7))
        interleave("scalar", ("p", 7), post[7], 0, 128)
        interleave("vector", ("p", 7), post[7], 128, N)
        for z in range(1, ZONE_TILES):
            finish("scalar", 0, z)
        quantize_post(6)
        quantize_post(7)
        for c in range(2):
            for z in range(ZONE_TILES):
                zones_pass(1, z, c)
        for z in range(ZONE_TILES):
            for c in range(2, CELL_PASSES):
                zones_pass(1, z, c)
            finish("vector" if z % 2 == 0 else "scalar", 1, z, 2 if z == ZONE_TILES - 1 else 1)
